import numpy as np
import ml_dtypes

BF16 = ml_dtypes.bfloat16


def bf(x):
    return np.asarray(x, np.float32).astype(BF16)


def f32(x):
    return np.asarray(x, np.float32)


def f64(x):
    return np.asarray(x).astype(np.float64)


def striped(idx):
    return np.tile(idx.reshape(-1, 16).T, (8, 1))


S, K, M, N = 256, 128, 128, 256


def setup_inputs():
    return {"table": bf(np.random.standard_normal((K, S))), "w": bf(np.random.standard_normal((K, M)) / np.sqrt(K)), "b": f32(0.5 * np.random.standard_normal((M, 1))), "offs": striped(np.random.permutation(S))}


def reference(table, w, b, offs):
    idx = offs[:16].T.reshape(-1)
    x = f64(table)[:, idx]
    y = f64(w).T @ x
    return y + f64(b)

@@ -1,0 +1,37 @@
+import concourse.mybir as mybir
+
+BF16, F32, U16 = mybir.dt.bfloat16, mybir.dt.float32, mybir.dt.uint16
+ADD = mybir.AluOpType.add
+
+K = 128
+M = 128
+S = 256
+N = 256
+
+FLOPS = 2 * K * M * N
+
+
+def tile_gather_matmul_kernel(tc, table, w, b, offs, out):
+    nc = tc.nc
+    with (
+        tc.tile_pool(name="held", bufs=1) as held,
+        tc.psum_pool(name="psum", bufs=1) as psum,
+    ):
+        offsets = held.tile([128, N // 16], U16, name="offsets")
+        tokens = held.tile([K, S], BF16, name="tokens")
+        weights = held.tile([K, M], BF16, name="weights")
+        bias = held.tile([M, 1], F32, name="bias")
+
+        nc.sync.dma_start(offsets[:], offs)
+        nc.scalar.dma_start(weights[:], w)
+        nc.sync.dma_start(tokens[:], table)
+        nc.scalar.dma_start(bias[:], b)
+
+        product = psum.tile([M, N], F32, name="product")
+        nc.tensor.matmul(
+            product[:], weights[:], tokens[:].indirect(offsets[:]), start=True, stop=True
+        )
+
+        result = held.tile([M, N], F32, name="result")
+        nc.vector.tensor_scalar(result[:], product[:], bias[:, 0:1], None, ADD)
+        nc.sync.dma_start(out, result[:])

@@ -8,6 +8,9 @@ M = 128
 S = 256
 N = 256
 
+PIECES = (128, 128)
+assert sum(PIECES) == N and all(width % 32 == 0 for width in PIECES)
+
 FLOPS = 2 * K * M * N
 
 
@@ -27,11 +30,18 @@ def tile_gather_matmul_kernel(tc, table, w, b, offs, out):
         nc.sync.dma_start(tokens[:], table)
         nc.scalar.dma_start(bias[:], b)
 
-        product = psum.tile([M, N], F32, name="product")
-        nc.tensor.matmul(
-            product[:], weights[:], tokens[:].indirect(offsets[:]), start=True, stop=True
-        )
-
-        result = held.tile([M, N], F32, name="result")
-        nc.vector.tensor_scalar(result[:], product[:], bias[:, 0:1], None, ADD)
-        nc.sync.dma_start(out, result[:])
+        store_queues = (nc.sync, nc.scalar)
+        first = 0
+        for piece, width in enumerate(PIECES):
+            product = psum.tile([M, width], F32, name=f"product{piece}")
+            nc.tensor.matmul(
+                product[:],
+                weights[:],
+                tokens[:].indirect(offsets[:, first // 16 : (first + width) // 16]),
+                start=True,
+                stop=True,
+            )
+            result = held.tile([M, width], F32, name=f"result{piece}")
+            nc.vector.tensor_scalar(result[:], product[:], bias[:, 0:1], None, ADD)
+            store_queues[piece % 2].dma_start(out[:, first : first + width], result[:])
+            first += width

@@ -8,10 +8,10 @@ M = 128
 S = 256
 N = 256
 
-PIECES = (128, 128)
-assert sum(PIECES) == N and all(width % 32 == 0 for width in PIECES)
-
 FLOPS = 2 * K * M * N
+
+WARMING_MATMULS = 4
+BANK = 512
 
 
 def tile_gather_matmul_kernel(tc, table, w, b, offs, out):
@@ -30,18 +30,17 @@ def tile_gather_matmul_kernel(tc, table, w, b, offs, out):
         nc.sync.dma_start(tokens[:], table)
         nc.scalar.dma_start(bias[:], b)
 
-        store_queues = (nc.sync, nc.scalar)
-        first = 0
-        for piece, width in enumerate(PIECES):
-            product = psum.tile([M, width], F32, name=f"product{piece}")
-            nc.tensor.matmul(
-                product[:],
-                weights[:],
-                tokens[:].indirect(offsets[:, first // 16 : (first + width) // 16]),
-                start=True,
-                stop=True,
-            )
-            result = held.tile([M, width], F32, name=f"result{piece}")
-            nc.vector.tensor_scalar(result[:], product[:], bias[:, 0:1], None, ADD)
-            store_queues[piece % 2].dma_start(out[:, first : first + width], result[:])
-            first += width
+        zeros = held.tile([K, BANK], BF16, name="zeros")
+        nc.vector.memset(zeros[:], 0.0)
+        unused = psum.tile([M, BANK], F32, name="unused")
+        for _ in range(WARMING_MATMULS):
+            nc.tensor.matmul(unused[:], zeros[:, 0:M], zeros[:], start=True, stop=True)
+
+        product = psum.tile([M, N], F32, name="product")
+        nc.tensor.matmul(
+            product[:], weights[:], tokens[:].indirect(offsets[:]), start=True, stop=True
+        )
+
+        result = held.tile([M, N], F32, name="result")
+        nc.vector.tensor_scalar(result[:], product[:], bias[:, 0:1], None, ADD)
+        nc.sync.dma_start(out, result[:])

@@ -10,9 +10,6 @@ N = 256
 
 FLOPS = 2 * K * M * N
 
-WARMING_MATMULS = 4
-BANK = 512
-
 
 def tile_gather_matmul_kernel(tc, table, w, b, offs, out):
     nc = tc.nc
@@ -26,15 +23,9 @@ def tile_gather_matmul_kernel(tc, table, w, b, offs, out):
         bias = held.tile([M, 1], F32, name="bias")
 
         nc.sync.dma_start(offsets[:], offs)
-        nc.scalar.dma_start(weights[:], w)
-        nc.sync.dma_start(tokens[:], table)
+        nc.scalar.dma_start(tokens[:], table)
+        nc.sync.dma_start(weights[:], w)
         nc.scalar.dma_start(bias[:], b)
-
-        zeros = held.tile([K, BANK], BF16, name="zeros")
-        nc.vector.memset(zeros[:], 0.0)
-        unused = psum.tile([M, BANK], F32, name="unused")
-        for _ in range(WARMING_MATMULS):
-            nc.tensor.matmul(unused[:], zeros[:, 0:M], zeros[:], start=True, stop=True)
 
         product = psum.tile([M, N], F32, name="product")
         nc.tensor.matmul(

@@ -22,9 +22,9 @@ def tile_gather_matmul_kernel(tc, table, w, b, offs, out):
         weights = held.tile([K, M], BF16, name="weights")
         bias = held.tile([M, 1], F32, name="bias")
 
-        nc.sync.dma_start(offsets[:], offs)
         nc.scalar.dma_start(tokens[:], table)
         nc.sync.dma_start(weights[:], w)
+        nc.sync.dma_start(offsets[:], offs)
         nc.scalar.dma_start(bias[:], b)
 
         product = psum.tile([M, N], F32, name="product")

@@ -7,6 +7,7 @@ K = 128
 M = 128
 S = 256
 N = 256
+HALF = N // 2
 
 FLOPS = 2 * K * M * N
 
@@ -33,5 +34,9 @@ def tile_gather_matmul_kernel(tc, table, w, b, offs, out):
         )
 
         result = held.tile([M, N], F32, name="result")
-        nc.vector.tensor_scalar(result[:], product[:], bias[:, 0:1], None, ADD)
-        nc.sync.dma_start(out, result[:])
+        for half in range(2):
+            columns = slice(half * HALF, (half + 1) * HALF)
+            nc.vector.tensor_scalar(
+                result[:, columns], product[:, columns], bias[:, 0:1], None, ADD
+            )
+            nc.sync.dma_start(out[:, columns], result[:, columns])

@@ -8,6 +8,7 @@ M = 128
 S = 256
 N = 256
 HALF = N // 2
+ROW_ALIGN = 256
 
 FLOPS = 2 * K * M * N
 
@@ -18,9 +19,10 @@ def tile_gather_matmul_kernel(tc, table, w, b, offs, out):
         tc.tile_pool(name="held", bufs=1) as held,
         tc.psum_pool(name="psum", bufs=1) as psum,
     ):
+        tokens = held.tile([K, S], BF16, name="tokens", align_bytes=ROW_ALIGN)
+        weights = held.tile([K, M], BF16, name="weights", align_bytes=ROW_ALIGN)
+        result = held.tile([M, N], F32, name="result", align_bytes=ROW_ALIGN)
         offsets = held.tile([128, N // 16], U16, name="offsets")
-        tokens = held.tile([K, S], BF16, name="tokens")
-        weights = held.tile([K, M], BF16, name="weights")
         bias = held.tile([M, 1], F32, name="bias")
 
         nc.scalar.dma_start(tokens[:], table)
@@ -33,7 +35,6 @@ def tile_gather_matmul_kernel(tc, table, w, b, offs, out):
             product[:], weights[:], tokens[:].indirect(offsets[:]), start=True, stop=True
         )
 
-        result = held.tile([M, N], F32, name="result")
         for half in range(2):
             columns = slice(half * HALF, (half + 1) * HALF)
             nc.vector.tensor_scalar(

@@ -17,7 +17,7 @@ def tile_gather_matmul_kernel(tc, table, w, b, offs, out):
     nc = tc.nc
     with (
         tc.tile_pool(name="held", bufs=1) as held,
-        tc.psum_pool(name="psum", bufs=1) as psum,
+        tc.psum_pool(name="psum", bufs=2) as psum,
     ):
         tokens = held.tile([K, S], BF16, name="tokens", align_bytes=ROW_ALIGN)
         weights = held.tile([K, M], BF16, name="weights", align_bytes=ROW_ALIGN)
@@ -30,14 +30,18 @@ def tile_gather_matmul_kernel(tc, table, w, b, offs, out):
         nc.sync.dma_start(offsets[:], offs)
         nc.scalar.dma_start(bias[:], b)
 
-        product = psum.tile([M, N], F32, name="product")
-        nc.tensor.matmul(
-            product[:], weights[:], tokens[:].indirect(offsets[:]), start=True, stop=True
-        )
-
         for half in range(2):
             columns = slice(half * HALF, (half + 1) * HALF)
+            entries = slice(half * HALF // 16, (half + 1) * HALF // 16)
+            product = psum.tile([M, HALF], F32, name="product")
+            nc.tensor.matmul(
+                product[:],
+                weights[:],
+                tokens[:].indirect(offsets[:, entries]),
+                start=True,
+                stop=True,
+            )
             nc.vector.tensor_scalar(
-                result[:, columns], product[:, columns], bias[:, 0:1], None, ADD
+                result[:, columns], product[:], bias[:, 0:1], None, ADD
             )
             nc.sync.dma_start(out[:, columns], result[:, columns])

@@ -1,7 +1,7 @@
 import concourse.mybir as mybir
 
 BF16, F32, U16 = mybir.dt.bfloat16, mybir.dt.float32, mybir.dt.uint16
-ADD = mybir.AluOpType.add
+IDENTITY = mybir.ActivationFunctionType.Identity
 
 K = 128
 M = 128
@@ -30,6 +30,10 @@ def tile_gather_matmul_kernel(tc, table, w, b, offs, out):
         nc.sync.dma_start(offsets[:], offs)
         nc.scalar.dma_start(bias[:], b)
 
+        idle = held.tile([M, 1], F32, name="idle")
+        nc.vector.memset(idle[:], 0.0)
+        nc.scalar.activation(idle[:], idle[:], IDENTITY)
+
         for half in range(2):
             columns = slice(half * HALF, (half + 1) * HALF)
             entries = slice(half * HALF // 16, (half + 1) * HALF // 16)
@@ -41,7 +45,7 @@ def tile_gather_matmul_kernel(tc, table, w, b, offs, out):
                 start=True,
                 stop=True,
             )
-            nc.vector.tensor_scalar(
-                result[:, columns], product[:], bias[:, 0:1], None, ADD
+            nc.scalar.activation(
+                result[:, columns], product[:], IDENTITY, bias=bias[:, 0:1]
             )
-            nc.sync.dma_start(out[:, columns], result[:, columns])
+            nc.scalar.dma_start(out[:, columns], result[:, columns])

@@ -48,4 +48,4 @@ def tile_gather_matmul_kernel(tc, table, w, b, offs, out):
             nc.scalar.activation(
                 result[:, columns], product[:], IDENTITY, bias=bias[:, 0:1]
             )
-            nc.scalar.dma_start(out[:, columns], result[:, columns])
+            nc.sync.dma_start(out[:, columns], result[:, columns])

@@ -1,6 +1,7 @@
 import concourse.mybir as mybir
 
 BF16, F32, U16 = mybir.dt.bfloat16, mybir.dt.float32, mybir.dt.uint16
+ADD = mybir.AluOpType.add
 IDENTITY = mybir.ActivationFunctionType.Identity
 
 K = 128
@@ -45,7 +46,12 @@ def tile_gather_matmul_kernel(tc, table, w, b, offs, out):
                 start=True,
                 stop=True,
             )
-            nc.scalar.activation(
-                result[:, columns], product[:], IDENTITY, bias=bias[:, 0:1]
-            )
+            if half == 0:
+                nc.vector.tensor_scalar(
+                    result[:, columns], product[:], bias[:, 0:1], None, ADD
+                )
+            else:
+                nc.scalar.activation(
+                    result[:, columns], product[:], IDENTITY, bias=bias[:, 0:1]
+                )
             nc.sync.dma_start(out[:, columns], result[:, columns])

@@ -29,11 +29,11 @@ def tile_gather_matmul_kernel(tc, table, w, b, offs, out):
         nc.scalar.dma_start(tokens[:], table)
         nc.sync.dma_start(weights[:], w)
         nc.sync.dma_start(offsets[:], offs)
-        nc.scalar.dma_start(bias[:], b)
 
         idle = held.tile([M, 1], F32, name="idle")
         nc.vector.memset(idle[:], 0.0)
         nc.scalar.activation(idle[:], idle[:], IDENTITY)
+        nc.scalar.dma_start(bias[:], b)
 
         for half in range(2):
             columns = slice(half * HALF, (half + 1) * HALF)

@@ -47,8 +47,11 @@ def tile_gather_matmul_kernel(tc, table, w, b, offs, out):
                 stop=True,
             )
             if half == 0:
-                nc.vector.tensor_scalar(
-                    result[:, columns], product[:], bias[:, 0:1], None, ADD
+                nc.vector.tensor_tensor(
+                    result[:, columns],
+                    product[:],
+                    bias[:].to_broadcast([M, HALF]),
+                    ADD,
                 )
             else:
                 nc.scalar.activation(

import concourse.mybir as mybir

BF16, F32, U16 = mybir.dt.bfloat16, mybir.dt.float32, mybir.dt.uint16
ADD = mybir.AluOpType.add
IDENTITY = mybir.ActivationFunctionType.Identity

K = 128
M = 128
S = 256
N = 256
HALF = N // 2
ROW_ALIGN = 256

FLOPS = 2 * K * M * N


def tile_gather_matmul_kernel(tc, table, w, b, offs, out):
    nc = tc.nc
    with (
        tc.tile_pool(name="held", bufs=1) as held,
        tc.psum_pool(name="psum", bufs=2) as psum,
    ):
        tokens = held.tile([K, S], BF16, name="tokens", align_bytes=ROW_ALIGN)
        weights = held.tile([K, M], BF16, name="weights", align_bytes=ROW_ALIGN)
        result = held.tile([M, N], F32, name="result", align_bytes=ROW_ALIGN)
        offsets = held.tile([128, N // 16], U16, name="offsets")
        bias = held.tile([M, 1], F32, name="bias")

        nc.scalar.dma_start(tokens[:], table)
        nc.sync.dma_start(weights[:], w)
        nc.sync.dma_start(offsets[:], offs)

        idle = held.tile([M, 1], F32, name="idle")
        nc.vector.memset(idle[:], 0.0)
        nc.scalar.activation(idle[:], idle[:], IDENTITY)
        nc.scalar.dma_start(bias[:], b)

        for half in range(2):
            columns = slice(half * HALF, (half + 1) * HALF)
            entries = slice(half * HALF // 16, (half + 1) * HALF // 16)
            product = psum.tile([M, HALF], F32, name="product")
            nc.tensor.matmul(
                product[:],
                weights[:],
                tokens[:].indirect(offsets[:, entries]),
                start=True,
                stop=True,
            )
            if half == 0:
                nc.vector.tensor_tensor(
                    result[:, columns],
                    product[:],
                    bias[:].to_broadcast([M, HALF]),
                    ADD,
                )
            else:
                nc.scalar.activation(
                    result[:, columns], product[:], IDENTITY, bias=bias[:, 0:1]
                )
            nc.sync.dma_start(out[:, columns], result[:, columns])
